import numpy as np
import ml_dtypes


def mxq(x, axis, fmt="e4m3"):
    dtype, down = {"e4m3": (ml_dtypes.float8_e4m3fn, 7), "e5m2": (ml_dtypes.float8_e5m2, 14)}[fmt]
    v = np.moveaxis(np.asarray(x, np.float32).astype(ml_dtypes.bfloat16).astype(np.float64), axis, -1)
    blocks = v.reshape(v.shape[:-1] + (-1, 32))
    amax = np.abs(blocks).max(-1, keepdims=True)
    byte = np.maximum(np.where(amax > 0, np.frexp(amax)[1] - 1 + 127, 0) - down, 1)
    scale = np.exp2(byte - 127.0)
    codes = (blocks / scale).astype(np.float32).astype(dtype).astype(np.float64)
    return np.moveaxis((codes * scale).reshape(v.shape), -1, axis)


WIDE = False


def mx_kscale(k):
    if not WIDE:
        return np.ones(k)
    levels = np.array([30, -30])
    if k % 512:
        return np.exp2(np.random.permutation(np.resize(levels, k // 32))).repeat(32)
    a = np.empty((k // 512, 16))
    for p in range(k // 512):
        a[p, :8] = np.random.permutation(np.resize(levels, 8))
        for g in range(8):
            far = levels[np.abs(levels - a[p, g]) >= 10]
            a[p, g + 8] = far[np.random.randint(len(far))]
    return np.exp2(a.ravel()).repeat(32)


BF16 = ml_dtypes.bfloat16


def bf(x):
    return np.asarray(x, np.float32).astype(BF16)


def f64(x):
    return np.asarray(x).astype(np.float64)


E2M1 = np.array([0.0, 0.5, 1.0, 1.5, 2.0, 3.0, 4.0, 6.0, -0.0, -0.5, -1.0, -1.5, -2.0, -3.0, -4.0, -6.0])


def pack_weight(w, fmt):
    k, n = w.shape
    w = f64(bf(w)).reshape(k // 32, 32, n)
    amax = np.abs(w).max(1)
    if fmt in ("e4m3", "e5m2"):
        byte = np.frexp(amax)[1] - 1 + 127 - (7 if fmt == "e4m3" else 14)
    else:
        mant, ex = np.frexp(amax / 6.0)
        byte = np.where(mant > 0.5, ex, ex - 1) + 127
    byte = np.clip(np.where(amax > 0, byte, 1), 1, 254)
    scaled = (w * np.exp2(127.0 - byte)[:, None, :]).reshape(k, n).astype(np.float32)
    by_word = np.ascontiguousarray(scaled.reshape(k // 512, 128, 4, n).transpose(0, 1, 3, 2))
    if fmt in ("e4m3", "e5m2"):
        words = by_word.astype(ml_dtypes.float8_e4m3fn if fmt == "e4m3" else ml_dtypes.float8_e5m2).view(np.uint8)
    else:
        c = by_word.astype(ml_dtypes.float4_e2m1fn).view(np.uint8) & 0xF
        words = c[..., 0::2] | (c[..., 1::2] << 4)
    return np.ascontiguousarray(words), np.ascontiguousarray(byte.astype(np.uint8).reshape(k // 512, 16, n))


def unpack_weight(words, scales, fmt):
    g, p, n, _ = words.shape
    if fmt in ("e4m3", "e5m2"):
        vals = np.ascontiguousarray(words).view(ml_dtypes.float8_e4m3fn if fmt == "e4m3" else ml_dtypes.float8_e5m2).astype(np.float64)
    else:
        nib = np.empty((g, p, n, 4), np.uint8)
        nib[..., 0::2] = words & 0xF
        nib[..., 1::2] = words >> 4
        vals = E2M1[nib]
    vals = vals * np.repeat(np.exp2(scales.astype(np.float64) - 127.0), 8, axis=1)[..., None]
    return vals.transpose(0, 1, 3, 2).reshape(g * 512, n)

def planes(Y):
    n, m = Y.shape
    b = f64(bf(Y)).reshape(n // 32, 32, m)
    amax = np.abs(b).max(1)
    byte = np.clip(np.where(amax > 0, np.frexp(amax)[1] - 1 + 127 - 7, 1), 1, 254)
    codes = (b * np.exp2(127.0 - byte)[:, None, :]).reshape(n, m).astype(np.float32).astype(ml_dtypes.float8_e4m3fn).view(np.uint8)
    words = codes.reshape(n // 512, 128, 4, m).transpose(0, 1, 3, 2)
    return np.ascontiguousarray(words), np.ascontiguousarray(byte.astype(np.uint8).reshape(n // 512, 16, m))


NAO, SPINS = 1024, 2
DIAGONAL, MIXING = 1.2, 0.35
FOCK_SIZE, POTENTIAL_SIZE = 0.2, 6.0

def symmetric_heavy_tailed(a):
    r = np.random.randn(NAO, NAO) * np.exp(0.6 * np.random.randn(NAO, NAO))
    return FOCK_SIZE * (r + r.T) * a[:, None] * a[None, :]

def setup_inputs():
    s = mx_kscale(NAO)
    w = np.random.randn(NAO, NAO)
    x = DIAGONAL * np.eye(NAO) + MIXING * (w + w.T) / np.sqrt(NAO)
    s_half = np.linalg.inv(x)
    a = np.exp(0.7 * np.random.randn(NAO))
    f = np.stack([symmetric_heavy_tailed(a) for z in range(SPINS)])
    f = np.moveaxis(f, 1, 0).reshape(NAO, SPINS * NAO)
    f_words, f_scales = pack_weight(f * s[:, None], "e5m2")
    v = POTENTIAL_SIZE * np.random.randn(SPINS, NAO)
    return {"f_words": f_words, "f_scales": f_scales, "x": bf(x / s[:, None]),
            "s_half": bf(s_half), "v": bf(v)}

def reference(f_words, f_scales, x, s_half, v):
    F = unpack_weight(f_words, f_scales, "e5m2")
    fx = (F.T @ mxq(f64(x), 0, "e4m3")).reshape(SPINS, NAO, NAO)
    y = fx + f64(s_half) * f64(v)[:, None, :]
    Y = np.moveaxis(y, 1, 0).reshape(NAO, SPINS * NAO)
    words, scales = planes(Y)
    return y, words, scales

@@ -1,0 +1,242 @@
+from contextlib import ExitStack
+
+import concourse.mybir as mybir
+from concourse.masks import make_identity
+
+F32 = mybir.dt.float32
+BF16 = mybir.dt.bfloat16
+I32 = mybir.dt.int32
+U32 = mybir.dt.uint32
+U8 = mybir.dt.uint8
+E4M3X4 = mybir.dt.float8_e4m3fn_x4
+E5M2X4 = mybir.dt.float8_e5m2_x4
+MULT = mybir.AluOpType.mult
+ADD = mybir.AluOpType.add
+
+NAO = 1024
+SPINS = 2
+P = 128
+PACK = 4
+SPAN = P * PACK
+PASSES = NAO // SPAN
+ROW_GROUPS = NAO // SPAN
+CHUNK = 256
+CHUNKS = NAO // CHUNK
+HALVES = CHUNK // P
+STEPS = CHUNKS * ROW_GROUPS
+UNITS = [(z, h) for z in range(SPINS) for h in range(HALVES)]
+
+FLOPS = 2 * NAO * NAO * SPINS * NAO
+
+
+def tile_loewdin_half_fock_k2_kernel(tc, f_words, f_scales, x, s_half, v, out_0, out_1, out_2):
+    nc = tc.nc
+    with ExitStack() as ctx:
+        keep = ctx.enter_context(tc.tile_pool(name="keep", bufs=1))
+        work = ctx.enter_context(tc.tile_pool(name="work", bufs=2))
+        psum = ctx.enter_context(tc.psum_pool(name="psum", bufs=1))
+        ctx.enter_context(tc.manual_schedule())
+
+        f_words_hbm = f_words.rearrange("k p n t -> p k (n t)").bitcast(I32)
+        f_scales_hbm = f_scales.rearrange("k (q r) n -> r q k n", r=4).bitcast(I32)
+
+        x_raw, s_raw, f_codes, f_plane = {}, {}, {}, {}
+        x_codes, x_plane, x_grouped = {}, {}, {}
+        s_turned, y_rows, y_grouped, y_turned = {}, {}, {}, {}
+
+        def load_x(c, k):
+            x_raw[c, k] = keep.tile([P, PACK, CHUNK], BF16, name="x_raw_%d_%d" % (c, k))
+            rows = x[k * SPAN : (k + 1) * SPAN, c * CHUNK : (c + 1) * CHUNK]
+            nc.sync.dma_start(out=x_raw[c, k][:], in_=rows.rearrange("(p t) j -> p t j", t=PACK))
+
+        def load_s(step):
+            c, g = divmod(step, ROW_GROUPS)
+            s_raw[step] = keep.tile([P, PACK, CHUNK], BF16, name="s_raw_%d" % step)
+            rows = s_half[g * SPAN : (g + 1) * SPAN, c * CHUNK : (c + 1) * CHUNK]
+            nc.sync.dma_start(out=s_raw[step][:], in_=rows.rearrange("(p t) j -> p t j", t=PACK))
+
+        def load_f(z, g):
+            f_codes[z, g] = keep.tile([P, PASSES, SPAN], U32, name="f_codes_%d_%d" % (z, g), align_bytes=64)
+            n0 = z * NAO + g * SPAN
+            nc.sync.dma_start(out=f_codes[z, g][:].bitcast(I32), in_=f_words_hbm[:, :, n0 : n0 + SPAN])
+
+        def load_f_scales(z):
+            words = NAO // 4
+            for r in range(4):
+                nc.sync.dma_start(
+                    out=f_plane[z][:].bitcast(I32)[r:P:32, :, :],
+                    in_=f_scales_hbm[r][:, :, z * words : (z + 1) * words],
+                )
+
+        def group_x_vector(c, k):
+            x_grouped[c, k] = work.tile([P, CHUNK, PACK], BF16, name="x_grouped_v", align_bytes=64, bufs=3)
+            nc.vector.tensor_copy(
+                out=x_grouped[c, k][:].rearrange("p (c i) t -> p c t i", i=4),
+                in_=x_raw[c, k][:].rearrange("p t (c i) -> p c t i", i=4),
+            )
+
+        def group_x_gpsimd(c, k):
+            x_grouped[c, k] = work.tile([P, CHUNK, PACK], BF16, name="x_grouped_g", align_bytes=64, bufs=1)
+            nc.gpsimd.tensor_scalar(
+                x_grouped[c, k][:], x_raw[c, k][:].rearrange("p t j -> p j t"), 1.0, 0.0, op0=MULT, op1=ADD
+            )
+
+        def quantize_x(c, k):
+            x_codes[c, k] = keep.tile([P, CHUNK], U32, name="x_codes_%d_%d" % (c, k), align_bytes=64)
+            x_plane[c, k] = keep.tile([P, CHUNK], U8, name="x_plane_%d_%d" % (c, k), align_bytes=64)
+            nc.vector.quantize_mx(
+                out=x_codes[c, k][:].bitcast(E4M3X4),
+                scales=x_plane[c, k][:],
+                in_=x_grouped[c, k][:].rearrange("p j t -> p (j t)"),
+            )
+
+        def turn_s(step, bank_tag):
+            bank = psum.tile([P, HALVES, PACK, P], BF16, name="s_bank", tag=bank_tag)
+            for h in range(HALVES):
+                for t in range(PACK):
+                    nc.tensor.transpose(bank[:, h, t, :], s_raw[step][:, t, h * P : (h + 1) * P], ident_bf16[:])
+            s_turned[step] = work.tile([P, HALVES, PACK, P], BF16, name="s_turned", bufs=2)
+            nc.scalar.copy(
+                out=s_turned[step][:].rearrange("p h t i -> p (h t i)"), in_=bank[:].rearrange("p h t i -> p (h t i)")
+            )
+
+        def multiply(step, u):
+            c, g = divmod(step, ROW_GROUPS)
+            z, h = UNITS[u]
+            acc = psum.tile([P, SPAN], F32, name="acc", tag="acc%d" % u)
+            for k in range(PASSES):
+                nc.tensor.matmul_mx(
+                    out=acc[:],
+                    lhsT=x_codes[c, k][:, h * P : (h + 1) * P].bitcast(E4M3X4),
+                    lhsT_scale=x_plane[c, k][:, h * P : (h + 1) * P],
+                    rhs=f_codes[z, g][:, k, :].bitcast(E5M2X4),
+                    rhs_scale=f_plane[z][:, k, g * SPAN : (g + 1) * SPAN],
+                    start=(k == 0),
+                    stop=(k == PASSES - 1),
+                )
+            return acc
+
+        def add_potential(step, u, acc):
+            c = step // ROW_GROUPS
+            z, h = UNITS[u]
+            column = z * (NAO // P) + c * HALVES + h
+            y_turned[step, u] = work.tile([P, PACK, P], F32, name="y_turned", bufs=6)
+            nc.vector.scalar_tensor_tensor(
+                out=y_turned[step, u][:],
+                in0=s_turned[step][:, h, :, :],
+                scalar=v_columns[:, column : column + 1],
+                in1=acc[:].rearrange("j (p t) -> j t p", t=PACK),
+                op0=MULT,
+                op1=ADD,
+            )
+
+        def turn_y(step, u):
+            z, h = UNITS[u]
+            bank = psum.tile([P, PACK, P], F32, name="y_bank", tag="turn%d" % u)
+            for t in range(PACK):
+                nc.tensor.transpose(bank[:, t, :], y_turned[step, u][:, t, :], ident_f32[:])
+            if h == 0:
+                y_rows[step, z] = work.tile([P, PACK, CHUNK], F32, name="y_rows", bufs=8)
+                y_grouped[step, z] = work.tile([P, CHUNK, PACK], BF16, name="y_grouped", bufs=6, align_bytes=64)
+            nc.scalar.copy(out=y_rows[step, z][:, :, h * P : (h + 1) * P], in_=bank[:])
+            if z == 1:
+                nc.scalar.copy(
+                    out=y_grouped[step, z][:, h * P : (h + 1) * P, :], in_=bank[:].rearrange("p t j -> p j t")
+                )
+
+        def store_y(step, z):
+            c, g = divmod(step, ROW_GROUPS)
+            rows = out_0[z, g * SPAN : (g + 1) * SPAN, c * CHUNK : (c + 1) * CHUNK]
+            nc.sync.dma_start(out=rows.rearrange("(p t) j -> p t j", t=PACK), in_=y_rows[step, z][:])
+
+        def make_planes(step):
+            c, g = divmod(step, ROW_GROUPS)
+            nc.vector.tensor_copy(
+                out=y_grouped[step, 0][:].rearrange("p (c i) t -> p c t i", i=4),
+                in_=y_rows[step, 0][:].rearrange("p t (c i) -> p c t i", i=4),
+            )
+            codes = work.tile([P, SPINS, CHUNK], U32, name="y_codes", bufs=4, align_bytes=64)
+            for z in (1, 0):
+                shift = 4 * (2 * z + c // 2)
+                n0 = (c % 2) * CHUNK
+                nc.vector.quantize_mx(
+                    out=codes[:, z, :].bitcast(E4M3X4),
+                    scales=y_plane[g][shift:P, n0 : n0 + CHUNK],
+                    in_=y_grouped[step, z][:].rearrange("p j t -> p (j t)"),
+                )
+            words = out_1[g].rearrange("p (z m) t -> p z (m t)", z=SPINS).bitcast(I32)
+            nc.sync.dma_start(out=words[:, :, c * CHUNK : (c + 1) * CHUNK], in_=codes[:].bitcast(I32))
+            if c == CHUNKS - 1:
+                for q in range(4):
+                    rows = out_2[g, 4 * q : 4 * q + 4, :].rearrange("r (k n) -> k r n", k=4).bitcast(I32)
+                    nc.sync.dma_start(out=rows, in_=y_plane[g][:].bitcast(I32)[32 * q : 32 * q + 16, :])
+
+        for z in range(SPINS):
+            f_plane[z] = keep.tile([P, PASSES, NAO], U8, name="f_plane_%d" % z, align_bytes=64)
+            nc.vector.memset(f_plane[z][:].rearrange("p k n -> p (k n)").bitcast(I32), 0)
+        y_plane = {}
+        for g in range(ROW_GROUPS):
+            y_plane[g] = keep.tile([P, 2 * CHUNK], U8, name="y_plane_%d" % g, align_bytes=64)
+
+        v_rows = keep.tile([P, P], BF16)
+        nc.gpsimd.memset(v_rows[:], 0.0)
+        nc.gpsimd.dma_start(out=v_rows[0 : SPINS * NAO // P, :], in_=v.rearrange("z (b p) -> (z b) p", p=P))
+        ident_bf16 = keep.tile([P, P], BF16)
+        make_identity(nc, ident_bf16[:])
+        ident_f32 = keep.tile([P, P], F32)
+        make_identity(nc, ident_f32[:])
+
+        load_x(0, 0)
+        load_x(0, 1)
+        load_f(0, 0)
+        load_f_scales(0)
+        load_s(0)
+        load_f(1, 0)
+        load_f_scales(1)
+        load_x(1, 0)
+        load_s(1)
+        load_x(1, 1)
+        load_f(0, 1)
+        load_f(1, 1)
+        for step in range(2, STEPS):
+            if step < STEPS - 2:
+                load_x(step // 2 + 1, step % 2)
+            load_s(step)
+
+        v_bank = psum.tile([P, P], BF16, tag="turn1")
+        nc.tensor.transpose(v_bank[:], v_rows[:], ident_bf16[:])
+        v_columns = keep.tile([P, SPINS * NAO // P], F32)
+        nc.scalar.copy(out=v_columns[:], in_=v_bank[:, 0 : SPINS * NAO // P])
+
+        group_x_vector(0, 0)
+        group_x_vector(0, 1)
+        quantize_x(0, 0)
+        quantize_x(0, 1)
+        group_x_vector(1, 0)
+        quantize_x(1, 0)
+
+        for step in range(STEPS):
+            ahead = divmod(step + 3, PASSES)
+            if ahead[0] < CHUNKS:
+                group_x_gpsimd(*ahead)
+            if step == 0:
+                early = [multiply(0, 0), multiply(0, 1)]
+                turn_s(0, "turn0")
+                add_potential(0, 0, early[0])
+                add_potential(0, 1, early[1])
+                for u in (2, 3):
+                    add_potential(0, u, multiply(0, u))
+            else:
+                for u in range(len(UNITS)):
+                    add_potential(step, u, multiply(step, u))
+            if step > 0:
+                make_planes(step - 1)
+            if ahead[0] < CHUNKS:
+                quantize_x(*ahead)
+            if step + 1 < STEPS:
+                turn_s(step + 1, "acc0")
+            for u in range(len(UNITS)):
+                turn_y(step, u)
+                if UNITS[u][1] == HALVES - 1:
+                    store_y(step, UNITS[u][0])
+        make_planes(STEPS - 1)

@@ -24,7 +24,6 @@ CHUNK = 256
 CHUNKS = NAO // CHUNK
 HALVES = CHUNK // P
 STEPS = CHUNKS * ROW_GROUPS
-UNITS = [(z, h) for z in range(SPINS) for h in range(HALVES)]
 
 FLOPS = 2 * NAO * NAO * SPINS * NAO
 
@@ -43,6 +42,7 @@ def tile_loewdin_half_fock_k2_kernel(tc, f_words, f_scales, x, s_half, v, out_0,
         x_raw, s_raw, f_codes, f_plane = {}, {}, {}, {}
         x_codes, x_plane, x_grouped = {}, {}, {}
         s_turned, y_rows, y_grouped, y_turned = {}, {}, {}, {}
+        acc, y_bank = {}, {}
 
         def load_x(c, k):
             x_raw[c, k] = keep.tile([P, PACK, CHUNK], BF16, name="x_raw_%d_%d" % (c, k))
@@ -55,10 +55,18 @@ def tile_loewdin_half_fock_k2_kernel(tc, f_words, f_scales, x, s_half, v, out_0,
             rows = s_half[g * SPAN : (g + 1) * SPAN, c * CHUNK : (c + 1) * CHUNK]
             nc.sync.dma_start(out=s_raw[step][:], in_=rows.rearrange("(p t) j -> p t j", t=PACK))
 
-        def load_f(z, g):
-            f_codes[z, g] = keep.tile([P, PASSES, SPAN], U32, name="f_codes_%d_%d" % (z, g), align_bytes=64)
+        def load_f(z, g, passes):
+            for k in passes:
+                f_codes[z, g, k] = keep.tile([P, SPAN], U32, name="f_codes_%d_%d_%d" % (z, g, k), align_bytes=64)
+                n0 = z * NAO + g * SPAN
+                nc.sync.dma_start(out=f_codes[z, g, k][:].bitcast(I32), in_=f_words_hbm[:, k, n0 : n0 + SPAN])
+
+        def load_f_both(z, g):
+            both = keep.tile([P, PASSES, SPAN], U32, name="f_codes_%d_%d" % (z, g), align_bytes=64)
             n0 = z * NAO + g * SPAN
-            nc.sync.dma_start(out=f_codes[z, g][:].bitcast(I32), in_=f_words_hbm[:, :, n0 : n0 + SPAN])
+            nc.sync.dma_start(out=both[:].bitcast(I32), in_=f_words_hbm[:, :, n0 : n0 + SPAN])
+            for k in range(PASSES):
+                f_codes[z, g, k] = both[:, k, :]
 
         def load_f_scales(z):
             words = NAO // 4
@@ -100,76 +108,81 @@ def tile_loewdin_half_fock_k2_kernel(tc, f_words, f_scales, x, s_half, v, out_0,
                 out=s_turned[step][:].rearrange("p h t i -> p (h t i)"), in_=bank[:].rearrange("p h t i -> p (h t i)")
             )
 
-        def multiply(step, u):
+        def place(n):
+            step, z = divmod(n, SPINS)
             c, g = divmod(step, ROW_GROUPS)
-            z, h = UNITS[u]
-            acc = psum.tile([P, SPAN], F32, name="acc", tag="acc%d" % u)
-            for k in range(PASSES):
-                nc.tensor.matmul_mx(
-                    out=acc[:],
-                    lhsT=x_codes[c, k][:, h * P : (h + 1) * P].bitcast(E4M3X4),
-                    lhsT_scale=x_plane[c, k][:, h * P : (h + 1) * P],
-                    rhs=f_codes[z, g][:, k, :].bitcast(E5M2X4),
-                    rhs_scale=f_plane[z][:, k, g * SPAN : (g + 1) * SPAN],
-                    start=(k == 0),
-                    stop=(k == PASSES - 1),
-                )
-            return acc
+            return step, z, c, g
 
-        def add_potential(step, u, acc):
-            c = step // ROW_GROUPS
-            z, h = UNITS[u]
+        def mx_pass(n, h, k):
+            step, z, c, g = place(n)
+            if k == 0:
+                acc[n, h] = psum.tile([P, SPAN], F32, name="acc", tag="acc", bufs=4)
+            nc.tensor.matmul_mx(
+                out=acc[n, h][:],
+                lhsT=x_codes[c, k][:, h * P : (h + 1) * P].bitcast(E4M3X4),
+                lhsT_scale=x_plane[c, k][:, h * P : (h + 1) * P],
+                rhs=f_codes[z, g, k][:].bitcast(E5M2X4),
+                rhs_scale=f_plane[z][:, k, g * SPAN : (g + 1) * SPAN],
+                start=(k == 0),
+                stop=(k == PASSES - 1),
+            )
+
+        def add_potential(n, h):
+            step, z, c, g = place(n)
             column = z * (NAO // P) + c * HALVES + h
-            y_turned[step, u] = work.tile([P, PACK, P], F32, name="y_turned", bufs=6)
+            y_turned[n, h] = work.tile([P, PACK, P], F32, name="y_turned", bufs=6)
             nc.vector.scalar_tensor_tensor(
-                out=y_turned[step, u][:],
+                out=y_turned[n, h][:],
                 in0=s_turned[step][:, h, :, :],
                 scalar=v_columns[:, column : column + 1],
-                in1=acc[:].rearrange("j (p t) -> j t p", t=PACK),
+                in1=acc[n, h][:].rearrange("j (p t) -> j t p", t=PACK),
                 op0=MULT,
                 op1=ADD,
             )
 
-        def turn_y(step, u):
-            z, h = UNITS[u]
-            bank = psum.tile([P, PACK, P], F32, name="y_bank", tag="turn%d" % u)
+        def turn_y(n, h):
+            y_bank[n, h] = psum.tile([P, PACK, P], F32, name="y_bank", tag="turn", bufs=3)
             for t in range(PACK):
-                nc.tensor.transpose(bank[:, t, :], y_turned[step, u][:, t, :], ident_f32[:])
+                nc.tensor.transpose(y_bank[n, h][:, t, :], y_turned[n, h][:, t, :], ident_f32[:])
             if h == 0:
-                y_rows[step, z] = work.tile([P, PACK, CHUNK], F32, name="y_rows", bufs=8)
-                y_grouped[step, z] = work.tile([P, CHUNK, PACK], BF16, name="y_grouped", bufs=6, align_bytes=64)
-            nc.scalar.copy(out=y_rows[step, z][:, :, h * P : (h + 1) * P], in_=bank[:])
-            if z == 1:
-                nc.scalar.copy(
-                    out=y_grouped[step, z][:, h * P : (h + 1) * P, :], in_=bank[:].rearrange("p t j -> p j t")
-                )
+                y_rows[n] = work.tile([P, PACK, CHUNK], F32, name="y_rows", bufs=8)
+                y_grouped[n] = work.tile([P, CHUNK, PACK], BF16, name="y_grouped", bufs=4, align_bytes=64)
 
-        def store_y(step, z):
-            c, g = divmod(step, ROW_GROUPS)
-            rows = out_0[z, g * SPAN : (g + 1) * SPAN, c * CHUNK : (c + 1) * CHUNK]
-            nc.sync.dma_start(out=rows.rearrange("(p t) j -> p t j", t=PACK), in_=y_rows[step, z][:])
+        def copy_y(n, h):
+            nc.scalar.copy(out=y_rows[n][:, :, h * P : (h + 1) * P], in_=y_bank[n, h][:])
 
-        def make_planes(step):
-            c, g = divmod(step, ROW_GROUPS)
+        def round_from_bank(copy, n, h):
+            copy(out=y_grouped[n][:, h * P : (h + 1) * P, :], in_=y_bank[n, h][:].rearrange("p t j -> p j t"))
+
+        def round_from_rows(n, h):
             nc.vector.tensor_copy(
-                out=y_grouped[step, 0][:].rearrange("p (c i) t -> p c t i", i=4),
-                in_=y_rows[step, 0][:].rearrange("p t (c i) -> p c t i", i=4),
+                out=y_grouped[n][:, h * P : (h + 1) * P, :].rearrange("p (c i) t -> p c t i", i=4),
+                in_=y_rows[n][:, :, h * P : (h + 1) * P].rearrange("p t (c i) -> p c t i", i=4),
             )
-            codes = work.tile([P, SPINS, CHUNK], U32, name="y_codes", bufs=4, align_bytes=64)
-            for z in (1, 0):
-                shift = 4 * (2 * z + c // 2)
-                n0 = (c % 2) * CHUNK
-                nc.vector.quantize_mx(
-                    out=codes[:, z, :].bitcast(E4M3X4),
-                    scales=y_plane[g][shift:P, n0 : n0 + CHUNK],
-                    in_=y_grouped[step, z][:].rearrange("p j t -> p (j t)"),
-                )
-            words = out_1[g].rearrange("p (z m) t -> p z (m t)", z=SPINS).bitcast(I32)
-            nc.sync.dma_start(out=words[:, :, c * CHUNK : (c + 1) * CHUNK], in_=codes[:].bitcast(I32))
-            if c == CHUNKS - 1:
+
+        def store_y(n):
+            step, z, c, g = place(n)
+            rows = out_0[z, g * SPAN : (g + 1) * SPAN, c * CHUNK : (c + 1) * CHUNK]
+            nc.sync.dma_start(out=rows.rearrange("(p t) j -> p t j", t=PACK), in_=y_rows[n][:])
+
+        def quantize_y(n):
+            step, z, c, g = place(n)
+            codes = work.tile([P, CHUNK], U32, name="y_codes", bufs=6, align_bytes=64)
+            shift = 4 * (2 * z + c // 2)
+            n0 = (c % 2) * CHUNK
+            nc.vector.quantize_mx(
+                out=codes[:].bitcast(E4M3X4),
+                scales=y_plane[g][shift:P, n0 : n0 + CHUNK],
+                in_=y_grouped[n][:].rearrange("p j t -> p (j t)"),
+            )
+            words = out_1[g].rearrange("p m t -> p (m t)").bitcast(I32)
+            m0 = z * NAO + c * CHUNK
+            nc.sync.dma_start(out=words[:, m0 : m0 + CHUNK], in_=codes[:].bitcast(I32))
+            if c == CHUNKS - 1 and z == SPINS - 1:
                 for q in range(4):
                     rows = out_2[g, 4 * q : 4 * q + 4, :].rearrange("r (k n) -> k r n", k=4).bitcast(I32)
-                    nc.sync.dma_start(out=rows, in_=y_plane[g][:].bitcast(I32)[32 * q : 32 * q + 16, :])
+                    queue = nc.scalar if g == ROW_GROUPS - 1 and q % 2 == 1 else nc.sync
+                    queue.dma_start(out=rows, in_=y_plane[g][:].bitcast(I32)[32 * q : 32 * q + 16, :])
 
         for z in range(SPINS):
             f_plane[z] = keep.tile([P, PASSES, NAO], U8, name="f_plane_%d" % z, align_bytes=64)
@@ -188,55 +201,72 @@ def tile_loewdin_half_fock_k2_kernel(tc, f_words, f_scales, x, s_half, v, out_0,
 
         load_x(0, 0)
         load_x(0, 1)
-        load_f(0, 0)
+        load_f(0, 0, [0])
         load_f_scales(0)
+        load_f(0, 0, [1])
         load_s(0)
-        load_f(1, 0)
+        load_f_both(1, 0)
         load_f_scales(1)
-        load_x(1, 0)
         load_s(1)
+        load_x(1, 0)
+        load_f_both(0, 1)
         load_x(1, 1)
-        load_f(0, 1)
-        load_f(1, 1)
+        load_f_both(1, 1)
         for step in range(2, STEPS):
+            load_s(step)
             if step < STEPS - 2:
                 load_x(step // 2 + 1, step % 2)
-            load_s(step)
-
-        v_bank = psum.tile([P, P], BF16, tag="turn1")
-        nc.tensor.transpose(v_bank[:], v_rows[:], ident_bf16[:])
-        v_columns = keep.tile([P, SPINS * NAO // P], F32)
-        nc.scalar.copy(out=v_columns[:], in_=v_bank[:, 0 : SPINS * NAO // P])
 
         group_x_vector(0, 0)
         group_x_vector(0, 1)
         quantize_x(0, 0)
         quantize_x(0, 1)
-        group_x_vector(1, 0)
-        quantize_x(1, 0)
+        group_x_gpsimd(1, 0)
 
-        for step in range(STEPS):
-            ahead = divmod(step + 3, PASSES)
-            if ahead[0] < CHUNKS:
-                group_x_gpsimd(*ahead)
-            if step == 0:
-                early = [multiply(0, 0), multiply(0, 1)]
-                turn_s(0, "turn0")
-                add_potential(0, 0, early[0])
-                add_potential(0, 1, early[1])
-                for u in (2, 3):
-                    add_potential(0, u, multiply(0, u))
-            else:
-                for u in range(len(UNITS)):
-                    add_potential(step, u, multiply(step, u))
-            if step > 0:
-                make_planes(step - 1)
-            if ahead[0] < CHUNKS:
-                quantize_x(*ahead)
-            if step + 1 < STEPS:
-                turn_s(step + 1, "acc0")
-            for u in range(len(UNITS)):
-                turn_y(step, u)
-                if UNITS[u][1] == HALVES - 1:
-                    store_y(step, UNITS[u][0])
-        make_planes(STEPS - 1)
+        for k in range(PASSES):
+            for h in range(HALVES):
+                mx_pass(0, h, k)
+        v_bank = psum.tile([P, P], BF16, tag="turn", bufs=3)
+        nc.tensor.transpose(v_bank[:], v_rows[:], ident_bf16[:])
+        v_columns = keep.tile([P, SPINS * NAO // P], F32)
+        nc.scalar.copy(out=v_columns[:], in_=v_bank[:, 0 : SPINS * NAO // P])
+        turn_s(0, "s_bank")
+        for h in range(HALVES):
+            add_potential(0, h)
+
+        last = STEPS * SPINS - 1
+        for n in range(1, last + 1):
+            step, z, c, g = place(n)
+            if n >= 2:
+                round_from_rows(n - 2, 0)
+            if g == 1 and c + 1 < CHUNKS:
+                quantize_x(c + 1, z)
+                following = divmod(PASSES * (c + 1) + z + 1, PASSES)
+                if following[0] < CHUNKS:
+                    group_x_gpsimd(*following)
+            for h in range(HALVES):
+                for k in range(PASSES):
+                    mx_pass(n, h, k)
+                add_potential(n, h)
+            if n >= 2:
+                quantize_y(n - 2)
+            if z == 1 and step + 1 < STEPS:
+                turn_s(step + 1, "s_bank")
+            for h in range(HALVES):
+                turn_y(n - 1, h)
+                copy_y(n - 1, h)
+            if n < last:
+                round_from_bank(nc.scalar.copy, n - 1, 1)
+            store_y(n - 1)
+
+        turn_y(last, 0)
+        copy_y(last, 0)
+        turn_y(last, 1)
+        round_from_rows(last - 1, 0)
+        round_from_bank(nc.vector.tensor_copy, last, 1)
+        copy_y(last, 1)
+        store_y(last)
+        round_from_rows(last - 1, 1)
+        round_from_rows(last, 0)
+        quantize_y(last - 1)
+        quantize_y(last)

from contextlib import ExitStack

import concourse.mybir as mybir
from concourse.masks import make_identity

F32 = mybir.dt.float32
BF16 = mybir.dt.bfloat16
I32 = mybir.dt.int32
U32 = mybir.dt.uint32
U8 = mybir.dt.uint8
E4M3X4 = mybir.dt.float8_e4m3fn_x4
E5M2X4 = mybir.dt.float8_e5m2_x4
MULT = mybir.AluOpType.mult
ADD = mybir.AluOpType.add

NAO = 1024
SPINS = 2
P = 128
PACK = 4
SPAN = P * PACK
PASSES = NAO // SPAN
ROW_GROUPS = NAO // SPAN
CHUNK = 256
CHUNKS = NAO // CHUNK
HALVES = CHUNK // P
STEPS = CHUNKS * ROW_GROUPS

FLOPS = 2 * NAO * NAO * SPINS * NAO


def tile_loewdin_half_fock_k2_kernel(tc, f_words, f_scales, x, s_half, v, out_0, out_1, out_2):
    nc = tc.nc
    with ExitStack() as ctx:
        keep = ctx.enter_context(tc.tile_pool(name="keep", bufs=1))
        work = ctx.enter_context(tc.tile_pool(name="work", bufs=2))
        psum = ctx.enter_context(tc.psum_pool(name="psum", bufs=1))
        ctx.enter_context(tc.manual_schedule())

        f_words_hbm = f_words.rearrange("k p n t -> p k (n t)").bitcast(I32)
        f_scales_hbm = f_scales.rearrange("k (q r) n -> r q k n", r=4).bitcast(I32)

        x_raw, s_raw, f_codes, f_plane = {}, {}, {}, {}
        x_codes, x_plane, x_grouped = {}, {}, {}
        s_turned, y_rows, y_grouped, y_turned = {}, {}, {}, {}
        acc, y_bank = {}, {}

        def load_x(c, k):
            x_raw[c, k] = keep.tile([P, PACK, CHUNK], BF16, name="x_raw_%d_%d" % (c, k))
            rows = x[k * SPAN : (k + 1) * SPAN, c * CHUNK : (c + 1) * CHUNK]
            nc.sync.dma_start(out=x_raw[c, k][:], in_=rows.rearrange("(p t) j -> p t j", t=PACK))

        def load_s(step):
            c, g = divmod(step, ROW_GROUPS)
            s_raw[step] = keep.tile([P, PACK, CHUNK], BF16, name="s_raw_%d" % step)
            rows = s_half[g * SPAN : (g + 1) * SPAN, c * CHUNK : (c + 1) * CHUNK]
            nc.sync.dma_start(out=s_raw[step][:], in_=rows.rearrange("(p t) j -> p t j", t=PACK))

        def load_f(z, g, passes):
            for k in passes:
                f_codes[z, g, k] = keep.tile([P, SPAN], U32, name="f_codes_%d_%d_%d" % (z, g, k), align_bytes=64)
                n0 = z * NAO + g * SPAN
                nc.sync.dma_start(out=f_codes[z, g, k][:].bitcast(I32), in_=f_words_hbm[:, k, n0 : n0 + SPAN])

        def load_f_both(z, g):
            both = keep.tile([P, PASSES, SPAN], U32, name="f_codes_%d_%d" % (z, g), align_bytes=64)
            n0 = z * NAO + g * SPAN
            nc.sync.dma_start(out=both[:].bitcast(I32), in_=f_words_hbm[:, :, n0 : n0 + SPAN])
            for k in range(PASSES):
                f_codes[z, g, k] = both[:, k, :]

        def load_f_scales(z):
            words = NAO // 4
            for r in range(4):
                nc.sync.dma_start(
                    out=f_plane[z][:].bitcast(I32)[r:P:32, :, :],
                    in_=f_scales_hbm[r][:, :, z * words : (z + 1) * words],
                )

        def group_x_vector(c, k):
            x_grouped[c, k] = work.tile([P, CHUNK, PACK], BF16, name="x_grouped_v", align_bytes=64, bufs=3)
            nc.vector.tensor_copy(
                out=x_grouped[c, k][:].rearrange("p (c i) t -> p c t i", i=4),
                in_=x_raw[c, k][:].rearrange("p t (c i) -> p c t i", i=4),
            )

        def group_x_gpsimd(c, k):
            x_grouped[c, k] = work.tile([P, CHUNK, PACK], BF16, name="x_grouped_g", align_bytes=64, bufs=1)
            nc.gpsimd.tensor_scalar(
                x_grouped[c, k][:], x_raw[c, k][:].rearrange("p t j -> p j t"), 1.0, 0.0, op0=MULT, op1=ADD
            )

        def quantize_x(c, k):
            x_codes[c, k] = keep.tile([P, CHUNK], U32, name="x_codes_%d_%d" % (c, k), align_bytes=64)
            x_plane[c, k] = keep.tile([P, CHUNK], U8, name="x_plane_%d_%d" % (c, k), align_bytes=64)
            nc.vector.quantize_mx(
                out=x_codes[c, k][:].bitcast(E4M3X4),
                scales=x_plane[c, k][:],
                in_=x_grouped[c, k][:].rearrange("p j t -> p (j t)"),
            )

        def turn_s(step, bank_tag):
            bank = psum.tile([P, HALVES, PACK, P], BF16, name="s_bank", tag=bank_tag)
            for h in range(HALVES):
                for t in range(PACK):
                    nc.tensor.transpose(bank[:, h, t, :], s_raw[step][:, t, h * P : (h + 1) * P], ident_bf16[:])
            s_turned[step] = work.tile([P, HALVES, PACK, P], BF16, name="s_turned", bufs=2)
            nc.scalar.copy(
                out=s_turned[step][:].rearrange("p h t i -> p (h t i)"), in_=bank[:].rearrange("p h t i -> p (h t i)")
            )

        def place(n):
            step, z = divmod(n, SPINS)
            c, g = divmod(step, ROW_GROUPS)
            return step, z, c, g

        def mx_pass(n, h, k):
            step, z, c, g = place(n)
            if k == 0:
                acc[n, h] = psum.tile([P, SPAN], F32, name="acc", tag="acc", bufs=4)
            nc.tensor.matmul_mx(
                out=acc[n, h][:],
                lhsT=x_codes[c, k][:, h * P : (h + 1) * P].bitcast(E4M3X4),
                lhsT_scale=x_plane[c, k][:, h * P : (h + 1) * P],
                rhs=f_codes[z, g, k][:].bitcast(E5M2X4),
                rhs_scale=f_plane[z][:, k, g * SPAN : (g + 1) * SPAN],
                start=(k == 0),
                stop=(k == PASSES - 1),
            )

        def add_potential(n, h):
            step, z, c, g = place(n)
            column = z * (NAO // P) + c * HALVES + h
            y_turned[n, h] = work.tile([P, PACK, P], F32, name="y_turned", bufs=6)
            nc.vector.scalar_tensor_tensor(
                out=y_turned[n, h][:],
                in0=s_turned[step][:, h, :, :],
                scalar=v_columns[:, column : column + 1],
                in1=acc[n, h][:].rearrange("j (p t) -> j t p", t=PACK),
                op0=MULT,
                op1=ADD,
            )

        def turn_y(n, h):
            y_bank[n, h] = psum.tile([P, PACK, P], F32, name="y_bank", tag="turn", bufs=3)
            for t in range(PACK):
                nc.tensor.transpose(y_bank[n, h][:, t, :], y_turned[n, h][:, t, :], ident_f32[:])
            if h == 0:
                y_rows[n] = work.tile([P, PACK, CHUNK], F32, name="y_rows", bufs=8)
                y_grouped[n] = work.tile([P, CHUNK, PACK], BF16, name="y_grouped", bufs=4, align_bytes=64)

        def copy_y(n, h):
            nc.scalar.copy(out=y_rows[n][:, :, h * P : (h + 1) * P], in_=y_bank[n, h][:])

        def round_from_bank(copy, n, h):
            copy(out=y_grouped[n][:, h * P : (h + 1) * P, :], in_=y_bank[n, h][:].rearrange("p t j -> p j t"))

        def round_from_rows(n, h):
            nc.vector.tensor_copy(
                out=y_grouped[n][:, h * P : (h + 1) * P, :].rearrange("p (c i) t -> p c t i", i=4),
                in_=y_rows[n][:, :, h * P : (h + 1) * P].rearrange("p t (c i) -> p c t i", i=4),
            )

        def store_y(n):
            step, z, c, g = place(n)
            rows = out_0[z, g * SPAN : (g + 1) * SPAN, c * CHUNK : (c + 1) * CHUNK]
            nc.sync.dma_start(out=rows.rearrange("(p t) j -> p t j", t=PACK), in_=y_rows[n][:])

        def quantize_y(n):
            step, z, c, g = place(n)
            codes = work.tile([P, CHUNK], U32, name="y_codes", bufs=6, align_bytes=64)
            shift = 4 * (2 * z + c // 2)
            n0 = (c % 2) * CHUNK
            nc.vector.quantize_mx(
                out=codes[:].bitcast(E4M3X4),
                scales=y_plane[g][shift:P, n0 : n0 + CHUNK],
                in_=y_grouped[n][:].rearrange("p j t -> p (j t)"),
            )
            words = out_1[g].rearrange("p m t -> p (m t)").bitcast(I32)
            m0 = z * NAO + c * CHUNK
            nc.sync.dma_start(out=words[:, m0 : m0 + CHUNK], in_=codes[:].bitcast(I32))
            if c == CHUNKS - 1 and z == SPINS - 1:
                for q in range(4):
                    rows = out_2[g, 4 * q : 4 * q + 4, :].rearrange("r (k n) -> k r n", k=4).bitcast(I32)
                    queue = nc.scalar if g == ROW_GROUPS - 1 and q % 2 == 1 else nc.sync
                    queue.dma_start(out=rows, in_=y_plane[g][:].bitcast(I32)[32 * q : 32 * q + 16, :])

        for z in range(SPINS):
            f_plane[z] = keep.tile([P, PASSES, NAO], U8, name="f_plane_%d" % z, align_bytes=64)
            nc.vector.memset(f_plane[z][:].rearrange("p k n -> p (k n)").bitcast(I32), 0)
        y_plane = {}
        for g in range(ROW_GROUPS):
            y_plane[g] = keep.tile([P, 2 * CHUNK], U8, name="y_plane_%d" % g, align_bytes=64)

        v_rows = keep.tile([P, P], BF16)
        nc.gpsimd.memset(v_rows[:], 0.0)
        nc.gpsimd.dma_start(out=v_rows[0 : SPINS * NAO // P, :], in_=v.rearrange("z (b p) -> (z b) p", p=P))
        ident_bf16 = keep.tile([P, P], BF16)
        make_identity(nc, ident_bf16[:])
        ident_f32 = keep.tile([P, P], F32)
        make_identity(nc, ident_f32[:])

        load_x(0, 0)
        load_x(0, 1)
        load_f(0, 0, [0])
        load_f_scales(0)
        load_f(0, 0, [1])
        load_s(0)
        load_f_both(1, 0)
        load_f_scales(1)
        load_s(1)
        load_x(1, 0)
        load_f_both(0, 1)
        load_x(1, 1)
        load_f_both(1, 1)
        for step in range(2, STEPS):
            load_s(step)
            if step < STEPS - 2:
                load_x(step // 2 + 1, step % 2)

        group_x_vector(0, 0)
        group_x_vector(0, 1)
        quantize_x(0, 0)
        quantize_x(0, 1)
        group_x_gpsimd(1, 0)

        for k in range(PASSES):
            for h in range(HALVES):
                mx_pass(0, h, k)
        v_bank = psum.tile([P, P], BF16, tag="turn", bufs=3)
        nc.tensor.transpose(v_bank[:], v_rows[:], ident_bf16[:])
        v_columns = keep.tile([P, SPINS * NAO // P], F32)
        nc.scalar.copy(out=v_columns[:], in_=v_bank[:, 0 : SPINS * NAO // P])
        turn_s(0, "s_bank")
        for h in range(HALVES):
            add_potential(0, h)

        last = STEPS * SPINS - 1
        for n in range(1, last + 1):
            step, z, c, g = place(n)
            if n >= 2:
                round_from_rows(n - 2, 0)
            if g == 1 and c + 1 < CHUNKS:
                quantize_x(c + 1, z)
                following = divmod(PASSES * (c + 1) + z + 1, PASSES)
                if following[0] < CHUNKS:
                    group_x_gpsimd(*following)
            for h in range(HALVES):
                for k in range(PASSES):
                    mx_pass(n, h, k)
                add_potential(n, h)
            if n >= 2:
                quantize_y(n - 2)
            if z == 1 and step + 1 < STEPS:
                turn_s(step + 1, "s_bank")
            for h in range(HALVES):
                turn_y(n - 1, h)
                copy_y(n - 1, h)
            if n < last:
                round_from_bank(nc.scalar.copy, n - 1, 1)
            store_y(n - 1)

        turn_y(last, 0)
        copy_y(last, 0)
        turn_y(last, 1)
        round_from_rows(last - 1, 0)
        round_from_bank(nc.vector.tensor_copy, last, 1)
        copy_y(last, 1)
        store_y(last)
        round_from_rows(last - 1, 1)
        round_from_rows(last, 0)
        quantize_y(last - 1)
        quantize_y(last)
